import numpy as np
CORES = [26,90,154,218,282,346,410,474]
N = 8
def setup_inputs(rng):
    return {"x1": rng.standard_normal((N, 128, 3), dtype=np.float32), "x2": rng.standard_normal((N, 128, 1), dtype=np.float32), "x3": rng.standard_normal((N, 128, 4), dtype=np.float32), "x4": rng.standard_normal((N, 128, 2), dtype=np.float32)}
def reference(x1, x2, x3, x4):
    out = {}
    s = x1.sum(axis=0, dtype=np.float64).astype(x1.dtype)
    out["y1"] = np.broadcast_to(s, (N,) + s.shape)
    s = x2.sum(axis=0, dtype=np.float64).astype(x2.dtype)
    out["y2"] = np.broadcast_to(s, (N,) + s.shape)
    s = x3.sum(axis=0, dtype=np.float64).astype(x3.dtype)
    out["y3"] = np.broadcast_to(s, (N,) + s.shape)
    s = x4.sum(axis=0, dtype=np.float64).astype(x4.dtype)
    out["y4"] = np.broadcast_to(s, (N,) + s.shape)
    return out

@@ -1,0 +1,65 @@
+from concourse.bass import DstId, RemoteDMATransfer
+from concourse.mybir import AluOpType
+
+W = 2
+SLOT = 640
+NB = 5
+ROWS = {"1": (0, 192), "2": (192, 256), "3": (256, 512), "4": (512, 640)}
+
+SCRATCH = {
+    "slot": ("dram", [4 * SLOT, W], "float32"),
+    "near": ("dram", [SLOT, W], "float32"),
+    "far": ("dram", [SLOT, W], "float32"),
+}
+SEMAPHORES = ["ld", "arr1", "arr2", "sent", "acc", "st"]
+
+
+def rank_program(g, core, T, topo):
+    rank = T.rank_of(core)
+    if rank is None:
+        return
+    cores = list(T.cores)
+    my_rack = topo.rack(topo.host(core))
+    rack_cores = [c for c in cores if topo.rack(topo.host(c)) == my_rack]
+    me = rack_cores.index(core)
+    peers = [c for c in rack_cores if c != core]
+    neighbour = [c for c in peers if topo.host(c) == topo.host(core)][0]
+    partner = [c for c in cores if topo.rack(topo.host(c)) != my_rack and topo.chip(c) == topo.chip(core)
+               and topo.may_write(core, c)][0]
+
+    def dst(c):
+        rid, pid = topo.addr(c, core)
+        return DstId(rid=rid, pnc=pid)
+
+    def blk(t, j, b):
+        r = j * SLOT + b * 128
+        return t[r:r + 128, :]
+
+    queues = {"1": g.scalar, "2": g.sync, "3": g.sync, "4": g.scalar}
+    for k in "3142":
+        a, b = ROWS[k]
+        queues[k].dma_start(T.slot[me * SLOT + a:me * SLOT + b, :], T["x" + k][:]).then_inc(T.sem.ld, 16)
+    g.wait_ge(T.sem.ld, 64)
+
+    g.remote_dma_fused([RemoteDMATransfer(
+        dst_ids=[dst(c) for c in peers], dma_engine_mask=1 << b, remote_sem=T.sem.arr1,
+        srcs=[blk(T.slot, me, b)], dsts=[blk(T.slot, me, b) for c in peers], alu_op=0)
+        for b in range(NB)], local_sem=T.sem.sent)
+    g.wait_ge(T.sem.arr1, 3 * NB)
+
+    g.remote_dma_fused([RemoteDMATransfer(
+        dst_ids=[dst(partner), dst(neighbour)], dma_engine_mask=1 << b, remote_sem=T.sem.arr2,
+        srcs=[blk(T.slot, j, b) for j in range(4)], dsts=[blk(T.far, 0, b), blk(T.near, 0, b)], alu_op=1)
+        for b in range(NB)], local_sem=T.sem.sent)
+    g.wait_ge(T.sem.arr2, 2 * NB)
+
+    g.dma_start(T.near[:], T.far[:], accum_op=AluOpType.add).then_inc(T.sem.acc, 16)
+
+    g.sync.wait_ge(T.sem.acc, 16)
+    g.scalar.wait_ge(T.sem.acc, 16)
+    for k in "3142":
+        a, b = ROWS[k]
+        queues[k].dma_start(T["y" + k][:], T.near[a:b, :]).then_inc(T.sem.st, 16)
+    g.wait_ge(T.sem.acc, 16)
+    g.wait_ge(T.sem.st, 64)
+    g.wait_ge(T.sem.sent, 2 * NB)

@@ -1,17 +1,26 @@
 from concourse.bass import DstId, RemoteDMATransfer
 from concourse.mybir import AluOpType
 
-W = 2
-SLOT = 640
-NB = 5
-ROWS = {"1": (0, 192), "2": (192, 256), "3": (256, 512), "4": (512, 640)}
+W = 10
+TILES = [
+    ("3", 0, 125, 64, 114, 0, 10),
+    ("1", 0, 120, 0, 36, 0, 10),
+    ("4", 8, 128, 40, 64, 0, 10),
+    ("2", 8, 128, 116, 128, 0, 10),
+    ("1", 120, 128, 36, 40, 0, 6),
+    ("4", 0, 8, 36, 40, 6, 10),
+    ("3", 125, 128, 114, 116, 0, 6),
+    ("2", 0, 8, 114, 116, 6, 10),
+]
 
 SCRATCH = {
-    "slot": ("dram", [4 * SLOT, W], "float32"),
-    "near": ("dram", [SLOT, W], "float32"),
-    "far": ("dram", [SLOT, W], "float32"),
+    "slot": ("dram", [4, 128, W], "float32"),
+    "near": ("dram", [128, W], "float32"),
+    "far": ("dram", [128, W], "float32"),
 }
 SEMAPHORES = ["ld", "arr1", "arr2", "sent", "acc", "st"]
+
+OFFCHIP = 0xFF
 
 
 def rank_program(g, core, T, topo):
@@ -31,35 +40,28 @@ def rank_program(g, core, T, topo):
         rid, pid = topo.addr(c, core)
         return DstId(rid=rid, pnc=pid)
 
-    def blk(t, j, b):
-        r = j * SLOT + b * 128
-        return t[r:r + 128, :]
+    queues = [g.sync, g.scalar]
 
-    queues = {"1": g.scalar, "2": g.sync, "3": g.sync, "4": g.scalar}
-    for k in "3142":
-        a, b = ROWS[k]
-        queues[k].dma_start(T.slot[me * SLOT + a:me * SLOT + b, :], T["x" + k][:]).then_inc(T.sem.ld, 16)
-    g.wait_ge(T.sem.ld, 64)
+    for i, (k, a, b, r0, r1, c0, c1) in enumerate(TILES):
+        queues[i % 2].dma_start(T.slot[me, r0:r1, c0:c1], T["x" + k][a:b, :]).then_inc(T.sem.ld, 16)
+    g.wait_ge(T.sem.ld, 16 * len(TILES))
 
     g.remote_dma_fused([RemoteDMATransfer(
-        dst_ids=[dst(c) for c in peers], dma_engine_mask=1 << b, remote_sem=T.sem.arr1,
-        srcs=[blk(T.slot, me, b)], dsts=[blk(T.slot, me, b) for c in peers], alu_op=0)
-        for b in range(NB)], local_sem=T.sem.sent)
-    g.wait_ge(T.sem.arr1, 3 * NB)
+        dst_ids=[dst(c) for c in peers], dma_engine_mask=OFFCHIP, remote_sem=T.sem.arr1,
+        srcs=[T.slot[me]], dsts=[T.slot[me] for c in peers], alu_op=0)], local_sem=T.sem.sent)
+    g.wait_ge(T.sem.arr1, 3 * 8)
 
     g.remote_dma_fused([RemoteDMATransfer(
-        dst_ids=[dst(partner), dst(neighbour)], dma_engine_mask=1 << b, remote_sem=T.sem.arr2,
-        srcs=[blk(T.slot, j, b) for j in range(4)], dsts=[blk(T.far, 0, b), blk(T.near, 0, b)], alu_op=1)
-        for b in range(NB)], local_sem=T.sem.sent)
-    g.wait_ge(T.sem.arr2, 2 * NB)
+        dst_ids=[dst(partner), dst(neighbour)], dma_engine_mask=OFFCHIP, remote_sem=T.sem.arr2,
+        srcs=[T.slot[j] for j in range(4)], dsts=[T.far[:], T.near[:]], alu_op=1)], local_sem=T.sem.sent)
+    g.wait_ge(T.sem.arr2, 2 * 8)
 
     g.dma_start(T.near[:], T.far[:], accum_op=AluOpType.add).then_inc(T.sem.acc, 16)
 
     g.sync.wait_ge(T.sem.acc, 16)
     g.scalar.wait_ge(T.sem.acc, 16)
-    for k in "3142":
-        a, b = ROWS[k]
-        queues[k].dma_start(T["y" + k][:], T.near[a:b, :]).then_inc(T.sem.st, 16)
+    for i, (k, a, b, r0, r1, c0, c1) in enumerate(TILES):
+        queues[i % 2].dma_start(T["y" + k][a:b, :], T.near[r0:r1, c0:c1]).then_inc(T.sem.st, 16)
     g.wait_ge(T.sem.acc, 16)
-    g.wait_ge(T.sem.st, 64)
-    g.wait_ge(T.sem.sent, 2 * NB)
+    g.wait_ge(T.sem.st, 16 * len(TILES))
+    g.wait_ge(T.sem.sent, 2 * 8)

from concourse.bass import DstId, RemoteDMATransfer
from concourse.mybir import AluOpType

W = 10
TILES = [
    ("3", 0, 125, 64, 114, 0, 10),
    ("1", 0, 120, 0, 36, 0, 10),
    ("4", 8, 128, 40, 64, 0, 10),
    ("2", 8, 128, 116, 128, 0, 10),
    ("1", 120, 128, 36, 40, 0, 6),
    ("4", 0, 8, 36, 40, 6, 10),
    ("3", 125, 128, 114, 116, 0, 6),
    ("2", 0, 8, 114, 116, 6, 10),
]

SCRATCH = {
    "slot": ("dram", [4, 128, W], "float32"),
    "near": ("dram", [128, W], "float32"),
    "far": ("dram", [128, W], "float32"),
}
SEMAPHORES = ["ld", "arr1", "arr2", "sent", "acc", "st"]

OFFCHIP = 0xFF


def rank_program(g, core, T, topo):
    rank = T.rank_of(core)
    if rank is None:
        return
    cores = list(T.cores)
    my_rack = topo.rack(topo.host(core))
    rack_cores = [c for c in cores if topo.rack(topo.host(c)) == my_rack]
    me = rack_cores.index(core)
    peers = [c for c in rack_cores if c != core]
    neighbour = [c for c in peers if topo.host(c) == topo.host(core)][0]
    partner = [c for c in cores if topo.rack(topo.host(c)) != my_rack and topo.chip(c) == topo.chip(core)
               and topo.may_write(core, c)][0]

    def dst(c):
        rid, pid = topo.addr(c, core)
        return DstId(rid=rid, pnc=pid)

    queues = [g.sync, g.scalar]

    for i, (k, a, b, r0, r1, c0, c1) in enumerate(TILES):
        queues[i % 2].dma_start(T.slot[me, r0:r1, c0:c1], T["x" + k][a:b, :]).then_inc(T.sem.ld, 16)
    g.wait_ge(T.sem.ld, 16 * len(TILES))

    g.remote_dma_fused([RemoteDMATransfer(
        dst_ids=[dst(c) for c in peers], dma_engine_mask=OFFCHIP, remote_sem=T.sem.arr1,
        srcs=[T.slot[me]], dsts=[T.slot[me] for c in peers], alu_op=0)], local_sem=T.sem.sent)
    g.wait_ge(T.sem.arr1, 3 * 8)

    g.remote_dma_fused([RemoteDMATransfer(
        dst_ids=[dst(partner), dst(neighbour)], dma_engine_mask=OFFCHIP, remote_sem=T.sem.arr2,
        srcs=[T.slot[j] for j in range(4)], dsts=[T.far[:], T.near[:]], alu_op=1)], local_sem=T.sem.sent)
    g.wait_ge(T.sem.arr2, 2 * 8)

    g.dma_start(T.near[:], T.far[:], accum_op=AluOpType.add).then_inc(T.sem.acc, 16)

    g.sync.wait_ge(T.sem.acc, 16)
    g.scalar.wait_ge(T.sem.acc, 16)
    for i, (k, a, b, r0, r1, c0, c1) in enumerate(TILES):
        queues[i % 2].dma_start(T["y" + k][a:b, :], T.near[r0:r1, c0:c1]).then_inc(T.sem.st, 16)
    g.wait_ge(T.sem.acc, 16)
    g.wait_ge(T.sem.st, 16 * len(TILES))
    g.wait_ge(T.sem.sent, 2 * 8)
